import numpy as np
import ml_dtypes


def mxq(x, axis, fmt="e4m3"):
    dtype, down = {"e4m3": (ml_dtypes.float8_e4m3fn, 7), "e5m2": (ml_dtypes.float8_e5m2, 14)}[fmt]
    v = np.moveaxis(np.asarray(x, np.float32).astype(ml_dtypes.bfloat16).astype(np.float64), axis, -1)
    blocks = v.reshape(v.shape[:-1] + (-1, 32))
    amax = np.abs(blocks).max(-1, keepdims=True)
    byte = np.maximum(np.where(amax > 0, np.frexp(amax)[1] - 1 + 127, 0) - down, 1)
    scale = np.exp2(byte - 127.0)
    codes = (blocks / scale).astype(np.float32).astype(dtype).astype(np.float64)
    return np.moveaxis((codes * scale).reshape(v.shape), -1, axis)


WIDE = False


def mx_kscale(k):
    if not WIDE:
        return np.ones(k)
    levels = np.array([10, -10, 5, -5, 0])
    if k % 512:
        return np.exp2(np.random.permutation(np.resize(levels, k // 32))).repeat(32)
    a = np.empty((k // 512, 16))
    for p in range(k // 512):
        a[p, :8] = np.random.permutation(np.resize(levels, 8))
        for g in range(8):
            far = levels[np.abs(levels - a[p, g]) >= 10]
            a[p, g + 8] = far[np.random.randint(len(far))]
    return np.exp2(a.ravel()).repeat(32)


def f64(x):
    return np.asarray(x).astype(np.float64)


def striped(idx):
    return np.tile(idx.reshape(-1, 16).T, (8, 1)).astype(np.uint16)


def unstriped(offs):
    return offs[:16].T.reshape(-1).astype(np.int64)


def striped8(idx):
    return np.concatenate([x.reshape(-1, 16).T for x in idx]).astype(np.uint16)


def runs(offs, k):
    lists = np.stack([offs[16 * r : 16 * r + 16].T.reshape(-1) for r in range(8)]).astype(np.int64)
    return lists[np.arange(k) % 512 // 64]


def pack_weight(w):
    k, n = w.shape
    w = f64(np.asarray(w, np.float32).astype(ml_dtypes.bfloat16)).reshape(k // 32, 32, n)
    amax = np.abs(w).max(1)
    byte = np.clip(np.where(amax > 0, np.frexp(amax)[1] - 1 + 127 - 7, 1), 1, 254)
    scaled = (w * np.exp2(127.0 - byte)[:, None, :]).reshape(k, n).astype(np.float32)
    words = np.ascontiguousarray(scaled.reshape(k // 512, 128, 4, n).transpose(0, 1, 3, 2)).astype(ml_dtypes.float8_e4m3fn).view(np.uint8)
    return words, np.ascontiguousarray(byte.astype(np.uint8).reshape(k // 512, 16, n))


def unpack_weight(words, scales):
    g, p, n, _ = words.shape
    vals = np.ascontiguousarray(words).view(ml_dtypes.float8_e4m3fn).astype(np.float64) * np.repeat(np.exp2(scales.astype(np.float64) - 127.0), 8, axis=1)[..., None]
    return vals.transpose(0, 1, 3, 2).reshape(g * 512, n)


def sigmoid(v):
    return 1.0 / (1.0 + np.exp(-np.maximum(v, -700.0)))

def planes(y):
    n, m = y.shape
    v = y.astype(np.float32).astype(ml_dtypes.bfloat16).astype(np.float64).reshape(n // 32, 32, m)
    top = np.abs(v).max(1)
    byte = np.clip(np.where(top > 0, np.frexp(top)[1] - 1 + 127 - 7, 1), 1, 254)
    codes = (v * np.exp2(127.0 - byte)[:, None, :]).reshape(n, m).astype(np.float32).astype(ml_dtypes.float8_e4m3fn).view(np.uint8)
    words = codes.reshape(n // 512, 128, 4, m).transpose(0, 1, 3, 2)
    return np.ascontiguousarray(words), np.ascontiguousarray(byte.astype(np.uint8).reshape(n // 512, 16, m))


K, T, S, H, C = 512, 2048, 512, 512, 512


def setup_inputs():
    n = np.random.standard_normal
    s = mx_kscale(K)[:, None]
    packed_xT = pack_weight(n((K, T)) * s)
    packed_w1 = pack_weight(n((K, H)) / np.sqrt(K) / s)
    packed_w2 = pack_weight(n((K, H)) / np.sqrt(K) / s)
    return {
        "x_words": packed_xT[0],
        "x_scales": packed_xT[1],
        "w1_words": packed_w1[0],
        "w1_scales": packed_w1[1],
        "w2_words": packed_w2[0],
        "w2_scales": packed_w2[1],
        "gs": (np.random.uniform(0.5, 1.5, (K, 1)) / s).astype(np.float32),
        "offs": striped(np.random.permutation(T)[:S]),
        "two": striped(np.random.permutation(T)[:S]),
        "n1": striped8(np.stack([np.random.permutation(S) for _ in range(8)])),
        "n2": striped8(np.stack([np.random.permutation(S) for _ in range(8)])),
        "cand": striped(np.random.permutation(T)[:C]),
        "n3": striped8(np.stack([np.random.permutation(S) for _ in range(8)])),
        "n4": striped8(np.stack([np.random.permutation(S) for _ in range(8)])),
    }


def reference(x_words, x_scales, w1_words, w1_scales, w2_words, w2_scales, gs, offs, two, n1, n2, cand, n3, n4):
    x_cand = unpack_weight(x_words, x_scales)[:, unstriped(cand)]
    xq = unpack_weight(x_words, x_scales)[:, unstriped(offs)]
    y = unpack_weight(w1_words, w1_scales).T @ xq
    x_two = unpack_weight(x_words, x_scales)[:, unstriped(two)]
    d = unpack_weight(w2_words, w2_scales).T @ x_two
    z = f64(gs) * (y + (sigmoid(d[np.arange(H)[:, None], runs(n2, H)] - d)) * (y[np.arange(H)[:, None], runs(n1, H)] - y))
    s = 0.0625 * ((x_cand.T @ mxq(z, 0, "e4m3")))
    st = s + s[np.arange(C)[:, None], runs(n3, C)]
    out_0 = st * (np.tanh(st[np.arange(C)[:, None], runs(n4, C)]))
    return (out_0,) + planes(out_0)

@@ -1,0 +1,234 @@
+from contextlib import ExitStack
+
+import concourse.mybir as mybir
+
+FLOPS = 805306368
+
+F32 = mybir.dt.float32
+BF16 = mybir.dt.bfloat16
+I32 = mybir.dt.int32
+U32 = mybir.dt.uint32
+U16 = mybir.dt.uint16
+U8 = mybir.dt.uint8
+FP8X4 = mybir.dt.float8_e4m3fn_x4
+ALU = mybir.AluOpType
+ACT = mybir.ActivationFunctionType
+
+P = 128
+PACK = 4
+T = 2048
+S = 512
+HALF = 256
+QUADS = 4
+FETCH_ON_S = ((3, 1),)
+A_SPANS = ((0, 256), (256, 512))
+B_SPANS = ((0, 256), (256, 512))
+D_ON_S = (0, 1)
+Y_ON_S = (0, 1, 2, 3)
+S_LAST_ON_S = (0,)
+CAST_ON_S = (0,)
+
+
+def tile_picked_twcpullbhopp_none_po_kernel(
+    tc, x_words, x_scales, w1_words, w1_scales, w2_words, w2_scales, gs, offs, two, n1, n2, cand, n3, n4, out_0, out_1, out_2
+):
+    nc = tc.nc
+    halves = [slice(h * HALF, (h + 1) * HALF) for h in range(2)]
+
+    def words_of(dram):
+        return dram[0].rearrange("p n t -> p (n t)").bitcast(I32)
+
+    with ExitStack() as ctx:
+        lists = ctx.enter_context(tc.tile_pool(name="lists", bufs=1))
+        sb = ctx.enter_context(tc.tile_pool(name="sb", bufs=1))
+        psum = ctx.enter_context(tc.psum_pool(name="psum", bufs=1))
+
+        def load_list(dram, name):
+            tile = lists.tile([P, S // 16], U16, name=name)
+            nc.sync.dma_start(tile[:], dram)
+            return tile
+
+        def load_scale_rows(queue, tile, dram):
+            rows = dram[0].bitcast(I32)
+            for q in range(QUADS):
+                queue.dma_start(out=tile[32 * q : 32 * q + 32, :].bitcast(I32), in_=rows[4 * q : 4 * q + 4, :].partition_broadcast(8))
+
+        xs = sb.tile([P, T], U8, name="xs", align_bytes=64)
+        xw = sb.tile([P, T], U32, name="xw", align_bytes=64)
+        ws1_raw = sb.tile([P, S], U8, name="ws1_raw", align_bytes=64)
+        ws2_raw = sb.tile([P, S], U8, name="ws2_raw", align_bytes=64)
+        w1_raw = sb.tile([P, S], U32, name="w1_raw", align_bytes=64)
+        w2_raw = sb.tile([P, S], U32, name="w2_raw", align_bytes=64)
+        gain = sb.tile([P, PACK], F32, name="gain")
+
+        two_l = load_list(two, "two_l")
+        load_scale_rows(nc.sync, xs, x_scales)
+        offs_l = load_list(offs, "offs_l")
+        nc.sync.dma_start(out=xw[:].bitcast(I32), in_=words_of(x_words))
+        nc.sync.dma_start(out=w2_raw[:].bitcast(I32), in_=words_of(w2_words))
+        load_scale_rows(nc.sync, ws2_raw, w2_scales)
+        n2_l = load_list(n2, "n2_l")
+        nc.sync.dma_start(out=w1_raw[:].bitcast(I32), in_=words_of(w1_words))
+        load_scale_rows(nc.sync, ws1_raw, w1_scales)
+        nc.sync.dma_start(out=gain[:], in_=gs.rearrange("(p t) o -> p (t o)", t=PACK))
+        cand_l = load_list(cand, "cand_l")
+        n1_l = load_list(n1, "n1_l")
+        n3_l = load_list(n3, "n3_l")
+        n4_l = load_list(n4, "n4_l")
+
+        def gather_packed(name, table, dtype, offsets, dealt, tag=None):
+            tile = sb.tile([P, S], dtype, name=name, tag=tag or name, align_bytes=64)
+            dst = tile[:].rearrange("p (t m) -> p m t", t=PACK) if dealt else tile[:]
+            nc.vector.tensor_copy(out=dst, in_=table[:].indirect(offsets[:]))
+            return tile
+
+        def deal_words(name, raw):
+            tile = sb.tile([P, S], U32, name=name, align_bytes=64)
+            nc.scalar.copy(
+                out=tile[:].rearrange("p (t c i) -> p c t i", t=PACK, i=4),
+                in_=raw[:].rearrange("p (c i t) -> p c t i", t=PACK, i=4),
+            )
+            return tile
+
+        def deal_scales(name, raw):
+            tile = sb.tile([P, S], U8, name=name, align_bytes=64)
+            nc.vector.tensor_copy(out=tile[:].rearrange("p (t m) -> p m t", t=PACK), in_=raw[:].rearrange("p (m t) -> p m t", t=PACK))
+            return tile
+
+        two_s = gather_packed("two_s", xs, U8, two_l, False)
+        offs_s = gather_packed("offs_s", xs, U8, offs_l, False)
+        two_w = gather_packed("two_w", xw, U32, two_l, False)
+        ws2 = deal_scales("ws2", ws2_raw)
+        w2 = deal_words("w2", w2_raw)
+        w1 = deal_words("w1", w1_raw)
+        offs_w = gather_packed("offs_w", xw, U32, offs_l, False, "ws2_raw")
+        ws1 = deal_scales("ws1", ws1_raw)
+        half_gain = sb.tile([P, PACK], F32, name="half_gain")
+        nc.vector.tensor_scalar(out=half_gain[:], in0=gain[:], scalar1=0.5, scalar2=None, op0=ALU.mult)
+
+        def product(bank, width, lhs, lhs_scale, rhs, rhs_scale):
+            acc = psum.tile([P, width], F32, name="acc", tag="bank%d" % bank)
+            nc.tensor.matmul_mx(out=acc[:], lhsT=lhs.bitcast(FP8X4), lhsT_scale=lhs_scale, rhs=rhs.bitcast(FP8X4), rhs_scale=rhs_scale, start=True, stop=True)
+            return acc
+
+        def cols(t):
+            return slice(t * P, (t + 1) * P)
+
+        d_ps = [product(t, S, w2[:, cols(t)], ws2[:, cols(t)], two_w[:], two_s[:]) for t in range(PACK)]
+        y_ps = [product(PACK + t, S, w1[:, cols(t)], ws1[:, cols(t)], offs_w[:], offs_s[:]) for t in range(PACK)]
+
+        d = [sb.tile([P, S], F32, name="d%d" % t) for t in range(PACK)]
+        y = [sb.tile([P, S], F32, name="y%d" % t) for t in range(PACK)]
+        s = [sb.tile([P, S], F32, name="s%d" % t) for t in range(PACK)]
+        st = [sb.tile([P, S], F32, name="st%d" % t) for t in range(PACK)]
+        th = [sb.tile([P, S], F32, name="th%d" % t) for t in range(PACK)]
+
+        def fetch(name, window, offsets, span):
+            tile = sb.tile([P, span.stop - span.start], F32, name=name)
+            nc.scalar.activation(out=tile[:], in_=window[:].indirect(offsets[:, span.start // 16 : span.stop // 16]), func=ACT.Copy)
+            return tile
+
+        def leave_psum(on_scalar, dst, src, scale):
+            if on_scalar:
+                nc.scalar.activation(out=dst, in_=src, func=ACT.Copy, scale=scale)
+            else:
+                nc.vector.tensor_scalar(out=dst, in0=src, scalar1=scale, scalar2=None, op0=ALU.mult)
+
+        z_words = sb.tile([P, S], U32, name="z_words", align_bytes=64)
+        z_scales = sb.tile([P, S], U8, name="z_scales", align_bytes=64)
+        cand_t = [gather_packed("cand_s", xs, U8, cand_l, True), gather_packed("cand_w", xw, U32, cand_l, True)]
+
+        def gate_args(c, span):
+            args = []
+            for t in range(PACK):
+                if c == 0:
+                    leave_psum(t in D_ON_S, d[t][:], d_ps[t][:], 1.0)
+                dg = fetch("dg%d%d" % (t, c), d[t], n2_l, span)
+                u = sb.tile([P, span.stop - span.start], F32, name="u%d%d" % (t, c))
+                nc.vector.tensor_tensor(out=u[:], in0=dg[:], in1=d[t][:, span], op=ALU.subtract)
+                args.append(u)
+            return args
+
+        def mix(c, span, args):
+            width = span.stop - span.start
+            far = sb.tile([P, PACK, width], F32, name="far%d" % c)
+            near = sb.tile([P, PACK, width], F32, name="near%d" % c)
+            for t in range(PACK):
+                if c == 0:
+                    leave_psum(t in Y_ON_S, y[t][:], y_ps[t][:], half_gain[:, t : t + 1])
+                g = sb.tile([P, width], F32, name="g%d%d" % (t, c))
+                nc.scalar.activation(out=g[:], in_=args[t][:], func=ACT.Tanh, scale=0.5)
+                yg = fetch("yg%d%d" % (t, c), y[t], n1_l, span)
+                nc.vector.scalar_tensor_tensor(out=near[:, t, :], in0=g[:], scalar=1.0, in1=y[t][:, span], op0=ALU.subtract, op1=ALU.mult)
+                nc.vector.scalar_tensor_tensor(out=far[:, t, :], in0=g[:], scalar=1.0, in1=yg[:], op0=ALU.add, op1=ALU.mult)
+            zb = sb.tile([P, width * PACK], BF16, name="zb%d" % c, align_bytes=64)
+            nc.vector.tensor_tensor(
+                out=zb[:].rearrange("p (c i t) -> p c t i", t=PACK, i=2),
+                in0=far[:].rearrange("p t (c i) -> p c t i", i=2),
+                in1=near[:].rearrange("p t (c i) -> p c t i", i=2),
+                op=ALU.subtract,
+            )
+            nc.vector.quantize_mx(out=z_words[:, span].bitcast(FP8X4), scales=z_scales[:, span], in_=zb[:])
+
+        def score(c, span):
+            last = c == len(A_SPANS) - 1
+            for t in range(PACK):
+                acc = product(PACK * (c % 2) + t, span.stop - span.start, cand_t[1][:, cols(t)], cand_t[0][:, cols(t)], z_words[:, span], z_scales[:, span])
+                leave_psum((not last) or t in S_LAST_ON_S, s[t][:, span], acc[:], 0.0625)
+
+        spans = [slice(a, b) for a, b in A_SPANS]
+        for c, span in enumerate(spans):
+            mix(c, span, gate_args(c, span))
+            if c > 0:
+                score(c - 1, spans[c - 1])
+        score(len(spans) - 1, spans[-1])
+
+        res = [sb.tile([P, PACK, b - a], F32, name="res%d" % a) for a, b in B_SPANS]
+        out_rows = out_0.rearrange("(p t) j -> p t j", t=PACK)
+
+        def hop(t):
+            for h in range(2):
+                sg = fetch("sg%d%d" % (t, h), s[t], n3_l, halves[h])
+                nc.vector.tensor_tensor(out=st[t][:, halves[h]], in0=sg[:], in1=s[t][:, halves[h]], op=ALU.add)
+
+        def squash(t):
+            for h in range(2):
+                nc.scalar.activation(out=th[t][:, halves[h]], in_=st[t][:, halves[h]], func=ACT.Tanh)
+
+        def finish(t, c):
+            a, b = B_SPANS[c]
+            if (t, c) in FETCH_ON_S:
+                tg = fetch("tg%d%d" % (t, c), th[t], n4_l, slice(a, b))
+                nc.vector.tensor_tensor(out=res[c][:, t, :], in0=tg[:], in1=st[t][:, a:b], op=ALU.mult)
+            else:
+                nc.vector.tensor_tensor(out=res[c][:, t, :], in0=th[t][:].indirect(n4_l[:, a // 16 : b // 16]), in1=st[t][:, a:b], op=ALU.mult)
+            nc.sync.dma_start(out=out_rows[:, t, a:b], in_=res[c][:, t, :])
+
+        o_words = sb.tile([P, S], U32, name="o_words", align_bytes=64)
+        o_scales = sb.tile([P, S], U8, name="o_scales", align_bytes=64)
+
+        def planes(c):
+            a, b = B_SPANS[c]
+            ob = sb.tile([P, (b - a) * PACK], BF16, name="ob%d" % c, align_bytes=64)
+            dst = ob[:].rearrange("p (c i t) -> p c t i", t=PACK, i=4)
+            src = res[c][:].rearrange("p t (c i) -> p c t i", i=4)
+            if c in CAST_ON_S:
+                nc.scalar.copy(out=dst, in_=src)
+            else:
+                nc.vector.tensor_copy(out=dst, in_=src)
+            nc.vector.quantize_mx(out=o_words[:, a:b].bitcast(FP8X4), scales=o_scales[:, a:b], in_=ob[:])
+            nc.sync.dma_start(out=words_of(out_1)[:, a:b], in_=o_words[:, a:b].bitcast(I32))
+
+        hop(0)
+        for t in range(PACK):
+            squash(t)
+            if t + 1 < PACK:
+                hop(t + 1)
+            for c in range(len(B_SPANS)):
+                finish(t, c)
+        for c in range(len(B_SPANS)):
+            planes(c)
+        scale_rows = out_2[0].bitcast(I32)
+        for q in range(QUADS):
+            queue = nc.sync if q % 2 == 0 else nc.scalar
+            queue.dma_start(out=scale_rows[4 * q : 4 * q + 4, :], in_=o_scales[32 * q : 32 * q + 4, :].bitcast(I32))

@@ -20,12 +20,16 @@ T = 2048
 S = 512
 HALF = 256
 QUADS = 4
-FETCH_ON_S = ((3, 1),)
+Q_SPANS = ((0, 256), (256, 512))
+Z_SPLIT = (1, 1)
+D_FUSED = ((0, 1), (1, 1), (2, 1), (3, 1))
+S_FUSED = ((0, 0), (1, 0), (2, 0), (3, 0))
+FETCH_ON_S = ((2, 1), (3, 1))
 A_SPANS = ((0, 256), (256, 512))
 B_SPANS = ((0, 256), (256, 512))
-D_ON_S = (0, 1)
+D_ON_S = (0, 1, 2)
 Y_ON_S = (0, 1, 2, 3)
-S_LAST_ON_S = (0,)
+S_LAST_ON_S = (0, 1, 2, 3)
 CAST_ON_S = (0,)
 
 
@@ -92,7 +96,7 @@ def tile_picked_twcpullbhopp_none_po_kernel(
 
         def deal_scales(name, raw):
             tile = sb.tile([P, S], U8, name=name, align_bytes=64)
-            nc.vector.tensor_copy(out=tile[:].rearrange("p (t m) -> p m t", t=PACK), in_=raw[:].rearrange("p (m t) -> p m t", t=PACK))
+            nc.vector.tensor_copy(out=tile[:].rearrange("p (t m) -> p t m", t=PACK), in_=raw[:].rearrange("p (m t) -> p t m", t=PACK))
             return tile
 
         two_s = gather_packed("two_s", xs, U8, two_l, False)
@@ -128,6 +132,14 @@ def tile_picked_twcpullbhopp_none_po_kernel(
             nc.scalar.activation(out=tile[:], in_=window[:].indirect(offsets[:, span.start // 16 : span.stop // 16]), func=ACT.Copy)
             return tile
 
+        def again(name, tile, span):
+            twin = sb.tile([P, span.stop - span.start], F32, name=name)
+            nc.sync.dma_start(out=twin[:], in_=tile[:, span])
+            return twin
+
+        d_again = {}
+        s_again = {}
+
         def leave_psum(on_scalar, dst, src, scale):
             if on_scalar:
                 nc.scalar.activation(out=dst, in_=src, func=ACT.Copy, scale=scale)
@@ -143,9 +155,14 @@ def tile_picked_twcpullbhopp_none_po_kernel(
             for t in range(PACK):
                 if c == 0:
                     leave_psum(t in D_ON_S, d[t][:], d_ps[t][:], 1.0)
-                dg = fetch("dg%d%d" % (t, c), d[t], n2_l, span)
+                    if (t, 1) in D_FUSED:
+                        d_again[t] = again("d_again%d" % t, d[t], halves[1])
                 u = sb.tile([P, span.stop - span.start], F32, name="u%d%d" % (t, c))
-                nc.vector.tensor_tensor(out=u[:], in0=dg[:], in1=d[t][:, span], op=ALU.subtract)
+                if (t, c) in D_FUSED:
+                    nc.vector.tensor_tensor(out=u[:], in0=d[t][:].indirect(n2_l[:, span.start // 16 : span.stop // 16]), in1=d_again[t][:], op=ALU.subtract)
+                else:
+                    dg = fetch("dg%d%d" % (t, c), d[t], n2_l, span)
+                    nc.vector.tensor_tensor(out=u[:], in0=dg[:], in1=d[t][:, span], op=ALU.subtract)
                 args.append(u)
             return args
 
@@ -175,21 +192,24 @@ def tile_picked_twcpullbhopp_none_po_kernel(
             for t in range(PACK):
                 acc = product(PACK * (c % 2) + t, span.stop - span.start, cand_t[1][:, cols(t)], cand_t[0][:, cols(t)], z_words[:, span], z_scales[:, span])
                 leave_psum((not last) or t in S_LAST_ON_S, s[t][:, span], acc[:], 0.0625)
+                if (t, c) in S_FUSED:
+                    s_again[t] = again("s_again%d" % t, s[t], span)
 
         spans = [slice(a, b) for a, b in A_SPANS]
         for c, span in enumerate(spans):
             mix(c, span, gate_args(c, span))
-            if c > 0:
-                score(c - 1, spans[c - 1])
-        score(len(spans) - 1, spans[-1])
+            score(c, span)
 
         res = [sb.tile([P, PACK, b - a], F32, name="res%d" % a) for a, b in B_SPANS]
         out_rows = out_0.rearrange("(p t) j -> p t j", t=PACK)
 
         def hop(t):
             for h in range(2):
-                sg = fetch("sg%d%d" % (t, h), s[t], n3_l, halves[h])
-                nc.vector.tensor_tensor(out=st[t][:, halves[h]], in0=sg[:], in1=s[t][:, halves[h]], op=ALU.add)
+                if (t, h) in S_FUSED:
+                    nc.vector.tensor_tensor(out=st[t][:, halves[h]], in0=s[t][:].indirect(n3_l[:, halves[h].start // 16 : halves[h].stop // 16]), in1=s_again[t][:], op=ALU.add)
+                else:
+                    sg = fetch("sg%d%d" % (t, h), s[t], n3_l, halves[h])
+                    nc.vector.tensor_tensor(out=st[t][:, halves[h]], in0=sg[:], in1=s[t][:, halves[h]], op=ALU.add)
 
         def squash(t):
             for h in range(2):
@@ -208,10 +228,10 @@ def tile_picked_twcpullbhopp_none_po_kernel(
         o_scales = sb.tile([P, S], U8, name="o_scales", align_bytes=64)
 
         def planes(c):
-            a, b = B_SPANS[c]
+            a, b = Q_SPANS[c]
             ob = sb.tile([P, (b - a) * PACK], BF16, name="ob%d" % c, align_bytes=64)
             dst = ob[:].rearrange("p (c i t) -> p c t i", t=PACK, i=4)
-            src = res[c][:].rearrange("p t (c i) -> p c t i", i=4)
+            src = res[a // HALF][:, :, a % HALF : a % HALF + b - a].rearrange("p t (c i) -> p c t i", i=4)
             if c in CAST_ON_S:
                 nc.scalar.copy(out=dst, in_=src)
             else:
@@ -226,7 +246,7 @@ def tile_picked_twcpullbhopp_none_po_kernel(
                 hop(t + 1)
             for c in range(len(B_SPANS)):
                 finish(t, c)
-        for c in range(len(B_SPANS)):
+        for c in range(len(Q_SPANS)):
             planes(c)
         scale_rows = out_2[0].bitcast(I32)
         for q in range(QUADS):

@@ -71,11 +71,11 @@ def tile_picked_twcpullbhopp_none_po_kernel(
         nc.sync.dma_start(out=xw[:].bitcast(I32), in_=words_of(x_words))
         nc.sync.dma_start(out=w2_raw[:].bitcast(I32), in_=words_of(w2_words))
         load_scale_rows(nc.sync, ws2_raw, w2_scales)
-        n2_l = load_list(n2, "n2_l")
+        cand_l = load_list(cand, "cand_l")
         nc.sync.dma_start(out=w1_raw[:].bitcast(I32), in_=words_of(w1_words))
+        n2_l = load_list(n2, "n2_l")
         load_scale_rows(nc.sync, ws1_raw, w1_scales)
         nc.sync.dma_start(out=gain[:], in_=gs.rearrange("(p t) o -> p (t o)", t=PACK))
-        cand_l = load_list(cand, "cand_l")
         n1_l = load_list(n1, "n1_l")
         n3_l = load_list(n3, "n3_l")
         n4_l = load_list(n4, "n4_l")
@@ -94,19 +94,19 @@ def tile_picked_twcpullbhopp_none_po_kernel(
             )
             return tile
 
-        def deal_scales(name, raw):
+        def deal_scales(engine, name, raw):
             tile = sb.tile([P, S], U8, name=name, align_bytes=64)
-            nc.vector.tensor_copy(out=tile[:].rearrange("p (t m) -> p t m", t=PACK), in_=raw[:].rearrange("p (m t) -> p t m", t=PACK))
+            engine.tensor_copy(out=tile[:].rearrange("p (t m) -> p t m", t=PACK), in_=raw[:].rearrange("p (m t) -> p t m", t=PACK))
             return tile
 
         two_s = gather_packed("two_s", xs, U8, two_l, False)
         offs_s = gather_packed("offs_s", xs, U8, offs_l, False)
         two_w = gather_packed("two_w", xw, U32, two_l, False)
-        ws2 = deal_scales("ws2", ws2_raw)
+        ws2 = deal_scales(nc.gpsimd, "ws2", ws2_raw)
         w2 = deal_words("w2", w2_raw)
         w1 = deal_words("w1", w1_raw)
-        offs_w = gather_packed("offs_w", xw, U32, offs_l, False, "ws2_raw")
-        ws1 = deal_scales("ws1", ws1_raw)
+        offs_w = gather_packed("offs_w", xw, U32, offs_l, False)
+        ws1 = deal_scales(nc.gpsimd, "ws1", ws1_raw)
         half_gain = sb.tile([P, PACK], F32, name="half_gain")
         nc.vector.tensor_scalar(out=half_gain[:], in0=gain[:], scalar1=0.5, scalar2=None, op0=ALU.mult)
 
@@ -155,8 +155,9 @@ def tile_picked_twcpullbhopp_none_po_kernel(
             for t in range(PACK):
                 if c == 0:
                     leave_psum(t in D_ON_S, d[t][:], d_ps[t][:], 1.0)
-                    if (t, 1) in D_FUSED:
-                        d_again[t] = again("d_again%d" % t, d[t], halves[1])
+                    for h in range(2):
+                        if (t, h) in D_FUSED:
+                            d_again[t] = again("d_again%d" % t, d[t], halves[h])
                 u = sb.tile([P, span.stop - span.start], F32, name="u%d%d" % (t, c))
                 if (t, c) in D_FUSED:
                     nc.vector.tensor_tensor(out=u[:], in0=d[t][:].indirect(n2_l[:, span.start // 16 : span.stop // 16]), in1=d_again[t][:], op=ALU.subtract)
@@ -178,27 +179,32 @@ def tile_picked_twcpullbhopp_none_po_kernel(
                 yg = fetch("yg%d%d" % (t, c), y[t], n1_l, span)
                 nc.vector.scalar_tensor_tensor(out=near[:, t, :], in0=g[:], scalar=1.0, in1=y[t][:, span], op0=ALU.subtract, op1=ALU.mult)
                 nc.vector.scalar_tensor_tensor(out=far[:, t, :], in0=g[:], scalar=1.0, in1=yg[:], op0=ALU.add, op1=ALU.mult)
-            zb = sb.tile([P, width * PACK], BF16, name="zb%d" % c, align_bytes=64)
-            nc.vector.tensor_tensor(
-                out=zb[:].rearrange("p (c i t) -> p c t i", t=PACK, i=2),
-                in0=far[:].rearrange("p t (c i) -> p c t i", i=2),
-                in1=near[:].rearrange("p t (c i) -> p c t i", i=2),
-                op=ALU.subtract,
-            )
-            nc.vector.quantize_mx(out=z_words[:, span].bitcast(FP8X4), scales=z_scales[:, span], in_=zb[:])
+            step = width // Z_SPLIT[c]
+            for a in range(0, width, step):
+                piece = slice(span.start + a, span.start + a + step)
+                zb = sb.tile([P, step * PACK], BF16, name="zb%d" % piece.start, align_bytes=64)
+                nc.vector.tensor_tensor(
+                    out=zb[:].rearrange("p (c i t) -> p c t i", t=PACK, i=2),
+                    in0=far[:, :, a : a + step].rearrange("p t (c i) -> p c t i", i=2),
+                    in1=near[:, :, a : a + step].rearrange("p t (c i) -> p c t i", i=2),
+                    op=ALU.subtract,
+                )
+                nc.vector.quantize_mx(out=z_words[:, piece].bitcast(FP8X4), scales=z_scales[:, piece], in_=zb[:])
+                score(c, piece)
+
+        scored = []
 
         def score(c, span):
-            last = c == len(A_SPANS) - 1
             for t in range(PACK):
-                acc = product(PACK * (c % 2) + t, span.stop - span.start, cand_t[1][:, cols(t)], cand_t[0][:, cols(t)], z_words[:, span], z_scales[:, span])
-                leave_psum((not last) or t in S_LAST_ON_S, s[t][:, span], acc[:], 0.0625)
+                acc = product(PACK * (len(scored) % 2) + t, span.stop - span.start, cand_t[1][:, cols(t)], cand_t[0][:, cols(t)], z_words[:, span], z_scales[:, span])
+                leave_psum(c == 0 or t in S_LAST_ON_S, s[t][:, span], acc[:], 0.0625)
                 if (t, c) in S_FUSED:
                     s_again[t] = again("s_again%d" % t, s[t], span)
+            scored.append(span)
 
         spans = [slice(a, b) for a, b in A_SPANS]
         for c, span in enumerate(spans):
             mix(c, span, gate_args(c, span))
-            score(c, span)
 
         res = [sb.tile([P, PACK, b - a], F32, name="res%d" % a) for a, b in B_SPANS]
         out_rows = out_0.rearrange("(p t) j -> p t j", t=PACK)
@@ -212,8 +218,7 @@ def tile_picked_twcpullbhopp_none_po_kernel(
                     nc.vector.tensor_tensor(out=st[t][:, halves[h]], in0=sg[:], in1=s[t][:, halves[h]], op=ALU.add)
 
         def squash(t):
-            for h in range(2):
-                nc.scalar.activation(out=th[t][:, halves[h]], in_=st[t][:, halves[h]], func=ACT.Tanh)
+            nc.scalar.activation(out=th[t][:], in_=st[t][:], func=ACT.Tanh)
 
         def finish(t, c):
             a, b = B_SPANS[c]

@@ -24,7 +24,7 @@ Q_SPANS = ((0, 256), (256, 512))
 Z_SPLIT = (1, 1)
 D_FUSED = ((0, 1), (1, 1), (2, 1), (3, 1))
 S_FUSED = ((0, 0), (1, 0), (2, 0), (3, 0))
-FETCH_ON_S = ((2, 1), (3, 1))
+FETCH_ON_S = ((0, 1), (1, 1), (2, 1), (3, 1))
 A_SPANS = ((0, 256), (256, 512))
 B_SPANS = ((0, 256), (256, 512))
 D_ON_S = (0, 1, 2)
@@ -71,11 +71,11 @@ def tile_picked_twcpullbhopp_none_po_kernel(
         nc.sync.dma_start(out=xw[:].bitcast(I32), in_=words_of(x_words))
         nc.sync.dma_start(out=w2_raw[:].bitcast(I32), in_=words_of(w2_words))
         load_scale_rows(nc.sync, ws2_raw, w2_scales)
-        cand_l = load_list(cand, "cand_l")
-        nc.sync.dma_start(out=w1_raw[:].bitcast(I32), in_=words_of(w1_words))
         n2_l = load_list(n2, "n2_l")
+        nc.sync.dma_start(out=w1_raw[:].bitcast(I32), in_=words_of(w1_words))
         load_scale_rows(nc.sync, ws1_raw, w1_scales)
         nc.sync.dma_start(out=gain[:], in_=gs.rearrange("(p t) o -> p (t o)", t=PACK))
+        cand_l = load_list(cand, "cand_l")
         n1_l = load_list(n1, "n1_l")
         n3_l = load_list(n3, "n3_l")
         n4_l = load_list(n4, "n4_l")
@@ -94,19 +94,19 @@ def tile_picked_twcpullbhopp_none_po_kernel(
             )
             return tile
 
-        def deal_scales(engine, name, raw):
+        def deal_scales(name, raw):
             tile = sb.tile([P, S], U8, name=name, align_bytes=64)
-            engine.tensor_copy(out=tile[:].rearrange("p (t m) -> p t m", t=PACK), in_=raw[:].rearrange("p (m t) -> p t m", t=PACK))
+            nc.vector.tensor_copy(out=tile[:].rearrange("p (t m) -> p t m", t=PACK), in_=raw[:].rearrange("p (m t) -> p t m", t=PACK))
             return tile
 
         two_s = gather_packed("two_s", xs, U8, two_l, False)
         offs_s = gather_packed("offs_s", xs, U8, offs_l, False)
         two_w = gather_packed("two_w", xw, U32, two_l, False)
-        ws2 = deal_scales(nc.gpsimd, "ws2", ws2_raw)
+        ws2 = deal_scales("ws2", ws2_raw)
         w2 = deal_words("w2", w2_raw)
         w1 = deal_words("w1", w1_raw)
-        offs_w = gather_packed("offs_w", xw, U32, offs_l, False)
-        ws1 = deal_scales(nc.gpsimd, "ws1", ws1_raw)
+        offs_w = gather_packed("offs_w", xw, U32, offs_l, False, "ws2_raw")
+        ws1 = deal_scales("ws1", ws1_raw)
         half_gain = sb.tile([P, PACK], F32, name="half_gain")
         nc.vector.tensor_scalar(out=half_gain[:], in0=gain[:], scalar1=0.5, scalar2=None, op0=ALU.mult)
 

@@ -184,9 +184,9 @@ def tile_picked_twcpullbhopp_none_po_kernel(
                 piece = slice(span.start + a, span.start + a + step)
                 zb = sb.tile([P, step * PACK], BF16, name="zb%d" % piece.start, align_bytes=64)
                 nc.vector.tensor_tensor(
-                    out=zb[:].rearrange("p (c i t) -> p c t i", t=PACK, i=2),
-                    in0=far[:, :, a : a + step].rearrange("p t (c i) -> p c t i", i=2),
-                    in1=near[:, :, a : a + step].rearrange("p t (c i) -> p c t i", i=2),
+                    out=zb[:].rearrange("p (c i t) -> p c t i", t=PACK, i=4),
+                    in0=far[:, :, a : a + step].rearrange("p t (c i) -> p c t i", i=4),
+                    in1=near[:, :, a : a + step].rearrange("p t (c i) -> p c t i", i=4),
                     op=ALU.subtract,
                 )
                 nc.vector.quantize_mx(out=z_words[:, piece].bitcast(FP8X4), scales=z_scales[:, piece], in_=zb[:])

from contextlib import ExitStack

import concourse.mybir as mybir

FLOPS = 805306368

F32 = mybir.dt.float32
BF16 = mybir.dt.bfloat16
I32 = mybir.dt.int32
U32 = mybir.dt.uint32
U16 = mybir.dt.uint16
U8 = mybir.dt.uint8
FP8X4 = mybir.dt.float8_e4m3fn_x4
ALU = mybir.AluOpType
ACT = mybir.ActivationFunctionType

P = 128
PACK = 4
T = 2048
S = 512
HALF = 256
QUADS = 4
Q_SPANS = ((0, 256), (256, 512))
Z_SPLIT = (1, 1)
D_FUSED = ((0, 1), (1, 1), (2, 1), (3, 1))
S_FUSED = ((0, 0), (1, 0), (2, 0), (3, 0))
FETCH_ON_S = ((0, 1), (1, 1), (2, 1), (3, 1))
A_SPANS = ((0, 256), (256, 512))
B_SPANS = ((0, 256), (256, 512))
D_ON_S = (0, 1, 2)
Y_ON_S = (0, 1, 2, 3)
S_LAST_ON_S = (0, 1, 2, 3)
CAST_ON_S = (0,)


def tile_picked_twcpullbhopp_none_po_kernel(
    tc, x_words, x_scales, w1_words, w1_scales, w2_words, w2_scales, gs, offs, two, n1, n2, cand, n3, n4, out_0, out_1, out_2
):
    nc = tc.nc
    halves = [slice(h * HALF, (h + 1) * HALF) for h in range(2)]

    def words_of(dram):
        return dram[0].rearrange("p n t -> p (n t)").bitcast(I32)

    with ExitStack() as ctx:
        lists = ctx.enter_context(tc.tile_pool(name="lists", bufs=1))
        sb = ctx.enter_context(tc.tile_pool(name="sb", bufs=1))
        psum = ctx.enter_context(tc.psum_pool(name="psum", bufs=1))

        def load_list(dram, name):
            tile = lists.tile([P, S // 16], U16, name=name)
            nc.sync.dma_start(tile[:], dram)
            return tile

        def load_scale_rows(queue, tile, dram):
            rows = dram[0].bitcast(I32)
            for q in range(QUADS):
                queue.dma_start(out=tile[32 * q : 32 * q + 32, :].bitcast(I32), in_=rows[4 * q : 4 * q + 4, :].partition_broadcast(8))

        xs = sb.tile([P, T], U8, name="xs", align_bytes=64)
        xw = sb.tile([P, T], U32, name="xw", align_bytes=64)
        ws1_raw = sb.tile([P, S], U8, name="ws1_raw", align_bytes=64)
        ws2_raw = sb.tile([P, S], U8, name="ws2_raw", align_bytes=64)
        w1_raw = sb.tile([P, S], U32, name="w1_raw", align_bytes=64)
        w2_raw = sb.tile([P, S], U32, name="w2_raw", align_bytes=64)
        gain = sb.tile([P, PACK], F32, name="gain")

        two_l = load_list(two, "two_l")
        load_scale_rows(nc.sync, xs, x_scales)
        offs_l = load_list(offs, "offs_l")
        nc.sync.dma_start(out=xw[:].bitcast(I32), in_=words_of(x_words))
        nc.sync.dma_start(out=w2_raw[:].bitcast(I32), in_=words_of(w2_words))
        load_scale_rows(nc.sync, ws2_raw, w2_scales)
        n2_l = load_list(n2, "n2_l")
        nc.sync.dma_start(out=w1_raw[:].bitcast(I32), in_=words_of(w1_words))
        load_scale_rows(nc.sync, ws1_raw, w1_scales)
        nc.sync.dma_start(out=gain[:], in_=gs.rearrange("(p t) o -> p (t o)", t=PACK))
        cand_l = load_list(cand, "cand_l")
        n1_l = load_list(n1, "n1_l")
        n3_l = load_list(n3, "n3_l")
        n4_l = load_list(n4, "n4_l")

        def gather_packed(name, table, dtype, offsets, dealt, tag=None):
            tile = sb.tile([P, S], dtype, name=name, tag=tag or name, align_bytes=64)
            dst = tile[:].rearrange("p (t m) -> p m t", t=PACK) if dealt else tile[:]
            nc.vector.tensor_copy(out=dst, in_=table[:].indirect(offsets[:]))
            return tile

        def deal_words(name, raw):
            tile = sb.tile([P, S], U32, name=name, align_bytes=64)
            nc.scalar.copy(
                out=tile[:].rearrange("p (t c i) -> p c t i", t=PACK, i=4),
                in_=raw[:].rearrange("p (c i t) -> p c t i", t=PACK, i=4),
            )
            return tile

        def deal_scales(name, raw):
            tile = sb.tile([P, S], U8, name=name, align_bytes=64)
            nc.vector.tensor_copy(out=tile[:].rearrange("p (t m) -> p t m", t=PACK), in_=raw[:].rearrange("p (m t) -> p t m", t=PACK))
            return tile

        two_s = gather_packed("two_s", xs, U8, two_l, False)
        offs_s = gather_packed("offs_s", xs, U8, offs_l, False)
        two_w = gather_packed("two_w", xw, U32, two_l, False)
        ws2 = deal_scales("ws2", ws2_raw)
        w2 = deal_words("w2", w2_raw)
        w1 = deal_words("w1", w1_raw)
        offs_w = gather_packed("offs_w", xw, U32, offs_l, False, "ws2_raw")
        ws1 = deal_scales("ws1", ws1_raw)
        half_gain = sb.tile([P, PACK], F32, name="half_gain")
        nc.vector.tensor_scalar(out=half_gain[:], in0=gain[:], scalar1=0.5, scalar2=None, op0=ALU.mult)

        def product(bank, width, lhs, lhs_scale, rhs, rhs_scale):
            acc = psum.tile([P, width], F32, name="acc", tag="bank%d" % bank)
            nc.tensor.matmul_mx(out=acc[:], lhsT=lhs.bitcast(FP8X4), lhsT_scale=lhs_scale, rhs=rhs.bitcast(FP8X4), rhs_scale=rhs_scale, start=True, stop=True)
            return acc

        def cols(t):
            return slice(t * P, (t + 1) * P)

        d_ps = [product(t, S, w2[:, cols(t)], ws2[:, cols(t)], two_w[:], two_s[:]) for t in range(PACK)]
        y_ps = [product(PACK + t, S, w1[:, cols(t)], ws1[:, cols(t)], offs_w[:], offs_s[:]) for t in range(PACK)]

        d = [sb.tile([P, S], F32, name="d%d" % t) for t in range(PACK)]
        y = [sb.tile([P, S], F32, name="y%d" % t) for t in range(PACK)]
        s = [sb.tile([P, S], F32, name="s%d" % t) for t in range(PACK)]
        st = [sb.tile([P, S], F32, name="st%d" % t) for t in range(PACK)]
        th = [sb.tile([P, S], F32, name="th%d" % t) for t in range(PACK)]

        def fetch(name, window, offsets, span):
            tile = sb.tile([P, span.stop - span.start], F32, name=name)
            nc.scalar.activation(out=tile[:], in_=window[:].indirect(offsets[:, span.start // 16 : span.stop // 16]), func=ACT.Copy)
            return tile

        def again(name, tile, span):
            twin = sb.tile([P, span.stop - span.start], F32, name=name)
            nc.sync.dma_start(out=twin[:], in_=tile[:, span])
            return twin

        d_again = {}
        s_again = {}

        def leave_psum(on_scalar, dst, src, scale):
            if on_scalar:
                nc.scalar.activation(out=dst, in_=src, func=ACT.Copy, scale=scale)
            else:
                nc.vector.tensor_scalar(out=dst, in0=src, scalar1=scale, scalar2=None, op0=ALU.mult)

        z_words = sb.tile([P, S], U32, name="z_words", align_bytes=64)
        z_scales = sb.tile([P, S], U8, name="z_scales", align_bytes=64)
        cand_t = [gather_packed("cand_s", xs, U8, cand_l, True), gather_packed("cand_w", xw, U32, cand_l, True)]

        def gate_args(c, span):
            args = []
            for t in range(PACK):
                if c == 0:
                    leave_psum(t in D_ON_S, d[t][:], d_ps[t][:], 1.0)
                    for h in range(2):
                        if (t, h) in D_FUSED:
                            d_again[t] = again("d_again%d" % t, d[t], halves[h])
                u = sb.tile([P, span.stop - span.start], F32, name="u%d%d" % (t, c))
                if (t, c) in D_FUSED:
                    nc.vector.tensor_tensor(out=u[:], in0=d[t][:].indirect(n2_l[:, span.start // 16 : span.stop // 16]), in1=d_again[t][:], op=ALU.subtract)
                else:
                    dg = fetch("dg%d%d" % (t, c), d[t], n2_l, span)
                    nc.vector.tensor_tensor(out=u[:], in0=dg[:], in1=d[t][:, span], op=ALU.subtract)
                args.append(u)
            return args

        def mix(c, span, args):
            width = span.stop - span.start
            far = sb.tile([P, PACK, width], F32, name="far%d" % c)
            near = sb.tile([P, PACK, width], F32, name="near%d" % c)
            for t in range(PACK):
                if c == 0:
                    leave_psum(t in Y_ON_S, y[t][:], y_ps[t][:], half_gain[:, t : t + 1])
                g = sb.tile([P, width], F32, name="g%d%d" % (t, c))
                nc.scalar.activation(out=g[:], in_=args[t][:], func=ACT.Tanh, scale=0.5)
                yg = fetch("yg%d%d" % (t, c), y[t], n1_l, span)
                nc.vector.scalar_tensor_tensor(out=near[:, t, :], in0=g[:], scalar=1.0, in1=y[t][:, span], op0=ALU.subtract, op1=ALU.mult)
                nc.vector.scalar_tensor_tensor(out=far[:, t, :], in0=g[:], scalar=1.0, in1=yg[:], op0=ALU.add, op1=ALU.mult)
            step = width // Z_SPLIT[c]
            for a in range(0, width, step):
                piece = slice(span.start + a, span.start + a + step)
                zb = sb.tile([P, step * PACK], BF16, name="zb%d" % piece.start, align_bytes=64)
                nc.vector.tensor_tensor(
                    out=zb[:].rearrange("p (c i t) -> p c t i", t=PACK, i=4),
                    in0=far[:, :, a : a + step].rearrange("p t (c i) -> p c t i", i=4),
                    in1=near[:, :, a : a + step].rearrange("p t (c i) -> p c t i", i=4),
                    op=ALU.subtract,
                )
                nc.vector.quantize_mx(out=z_words[:, piece].bitcast(FP8X4), scales=z_scales[:, piece], in_=zb[:])
                score(c, piece)

        scored = []

        def score(c, span):
            for t in range(PACK):
                acc = product(PACK * (len(scored) % 2) + t, span.stop - span.start, cand_t[1][:, cols(t)], cand_t[0][:, cols(t)], z_words[:, span], z_scales[:, span])
                leave_psum(c == 0 or t in S_LAST_ON_S, s[t][:, span], acc[:], 0.0625)
                if (t, c) in S_FUSED:
                    s_again[t] = again("s_again%d" % t, s[t], span)
            scored.append(span)

        spans = [slice(a, b) for a, b in A_SPANS]
        for c, span in enumerate(spans):
            mix(c, span, gate_args(c, span))

        res = [sb.tile([P, PACK, b - a], F32, name="res%d" % a) for a, b in B_SPANS]
        out_rows = out_0.rearrange("(p t) j -> p t j", t=PACK)

        def hop(t):
            for h in range(2):
                if (t, h) in S_FUSED:
                    nc.vector.tensor_tensor(out=st[t][:, halves[h]], in0=s[t][:].indirect(n3_l[:, halves[h].start // 16 : halves[h].stop // 16]), in1=s_again[t][:], op=ALU.add)
                else:
                    sg = fetch("sg%d%d" % (t, h), s[t], n3_l, halves[h])
                    nc.vector.tensor_tensor(out=st[t][:, halves[h]], in0=sg[:], in1=s[t][:, halves[h]], op=ALU.add)

        def squash(t):
            nc.scalar.activation(out=th[t][:], in_=st[t][:], func=ACT.Tanh)

        def finish(t, c):
            a, b = B_SPANS[c]
            if (t, c) in FETCH_ON_S:
                tg = fetch("tg%d%d" % (t, c), th[t], n4_l, slice(a, b))
                nc.vector.tensor_tensor(out=res[c][:, t, :], in0=tg[:], in1=st[t][:, a:b], op=ALU.mult)
            else:
                nc.vector.tensor_tensor(out=res[c][:, t, :], in0=th[t][:].indirect(n4_l[:, a // 16 : b // 16]), in1=st[t][:, a:b], op=ALU.mult)
            nc.sync.dma_start(out=out_rows[:, t, a:b], in_=res[c][:, t, :])

        o_words = sb.tile([P, S], U32, name="o_words", align_bytes=64)
        o_scales = sb.tile([P, S], U8, name="o_scales", align_bytes=64)

        def planes(c):
            a, b = Q_SPANS[c]
            ob = sb.tile([P, (b - a) * PACK], BF16, name="ob%d" % c, align_bytes=64)
            dst = ob[:].rearrange("p (c i t) -> p c t i", t=PACK, i=4)
            src = res[a // HALF][:, :, a % HALF : a % HALF + b - a].rearrange("p t (c i) -> p c t i", i=4)
            if c in CAST_ON_S:
                nc.scalar.copy(out=dst, in_=src)
            else:
                nc.vector.tensor_copy(out=dst, in_=src)
            nc.vector.quantize_mx(out=o_words[:, a:b].bitcast(FP8X4), scales=o_scales[:, a:b], in_=ob[:])
            nc.sync.dma_start(out=words_of(out_1)[:, a:b], in_=o_words[:, a:b].bitcast(I32))

        hop(0)
        for t in range(PACK):
            squash(t)
            if t + 1 < PACK:
                hop(t + 1)
            for c in range(len(B_SPANS)):
                finish(t, c)
        for c in range(len(Q_SPANS)):
            planes(c)
        scale_rows = out_2[0].bitcast(I32)
        for q in range(QUADS):
            queue = nc.sync if q % 2 == 0 else nc.scalar
            queue.dma_start(out=scale_rows[4 * q : 4 * q + 4, :], in_=o_scales[32 * q : 32 * q + 4, :].bitcast(I32))
